import numpy as np
import ml_dtypes

BF16 = ml_dtypes.bfloat16


def bf(x):
    return np.asarray(x, np.float32).astype(BF16)


def f32(x):
    return np.asarray(x, np.float32)


def f64(x):
    return np.asarray(x).astype(np.float64)


def striped(idx):
    return np.concatenate([l.reshape(-1, 16).T for l in idx])


def rows(idx, k):
    return np.tile(np.repeat(idx, 16, axis=0), (k // (16 * 8), 1))


def look(tab, idx):
    return np.take_along_axis(f64(tab), rows(idx, len(tab)), axis=1)


K, S, V, N = 256, 2048, 2048, 2048


def silu(v):
    return v / (1.0 + np.exp(-v))


def setup_inputs():
    return {"tab": f32(np.random.standard_normal((K, S))), "y": f32(np.random.standard_normal((K, V))), "offs": striped(np.stack([np.random.permutation(S)[:N] for _ in range(8)]))}


def reference(tab, y, offs):
    idx = np.stack([g.T.reshape(-1) for g in np.split(offs, 8)])
    t = look(tab, idx)
    x = silu(t) * f64(y)
    return x

@@ -1,0 +1,45 @@
+import concourse.mybir as mybir
+
+F32 = mybir.dt.float32
+U16 = mybir.dt.uint16
+SILU = mybir.ActivationFunctionType.Silu
+MULT = mybir.AluOpType.mult
+
+P = 128
+OFFSETS_PER_COL = 16
+PIECE = 512
+
+
+def tile_lookup_gate_silu_out_kernel(tc, tab, y, offs, out):
+    nc = tc.nc
+    rows, table_cols = tab.shape
+    n = y.shape[1]
+    blocks = rows // P
+    pieces = n // PIECE
+    piece_offset_cols = PIECE // OFFSETS_PER_COL
+
+    with (
+        tc.tile_pool(name="held", bufs=1) as held,
+        tc.tile_pool(name="work", bufs=blocks * pieces) as work,
+    ):
+        offsets = held.tile([P, n // OFFSETS_PER_COL], U16, name="offsets")
+        nc.sync.dma_start(offsets[:], offs)
+        windows = []
+        streams = []
+        for b in range(blocks):
+            window = held.tile([P, table_cols], F32, name=f"window{b}")
+            nc.sync.dma_start(window[:], tab[b * P : (b + 1) * P, :])
+            windows.append(window)
+            stream = held.tile([P, n], F32, name=f"stream{b}")
+            nc.sync.dma_start(stream[:], y[b * P : (b + 1) * P, :])
+            streams.append(stream)
+
+        for b in range(blocks):
+            for k in range(pieces):
+                cols = slice(k * PIECE, (k + 1) * PIECE)
+                piece_offsets = offsets[:, k * piece_offset_cols : (k + 1) * piece_offset_cols]
+                gate = work.tile([P, PIECE], F32, name="gate")
+                nc.scalar.activation(gate[:], windows[b][:].indirect(piece_offsets), SILU)
+                x = work.tile([P, PIECE], F32, name="x")
+                nc.vector.tensor_tensor(x[:], gate[:], streams[b][:, cols], MULT)
+                nc.sync.dma_start(out[b * P : (b + 1) * P, cols], x[:])

@@ -7,6 +7,7 @@ MULT = mybir.AluOpType.mult
 
 P = 128
 OFFSETS_PER_COL = 16
+WARM_COLS = 8
 PIECE = 512
 
 
@@ -22,6 +23,11 @@ def tile_lookup_gate_silu_out_kernel(tc, tab, y, offs, out):
         tc.tile_pool(name="held", bufs=1) as held,
         tc.tile_pool(name="work", bufs=blocks * pieces) as work,
     ):
+        zeros = held.tile([P, WARM_COLS], F32, name="zeros")
+        nc.vector.memset(zeros[:], 0.0)
+        warm = held.tile([P, WARM_COLS], F32, name="warm")
+        nc.scalar.activation(warm[:], zeros[:], SILU)
+
         offsets = held.tile([P, n // OFFSETS_PER_COL], U16, name="offsets")
         nc.sync.dma_start(offsets[:], offs)
         windows = []

@@ -8,6 +8,7 @@ MULT = mybir.AluOpType.mult
 P = 128
 OFFSETS_PER_COL = 16
 WARM_COLS = 8
+LAST_PARTS = 2
 PIECE = 512
 
 
@@ -21,7 +22,7 @@ def tile_lookup_gate_silu_out_kernel(tc, tab, y, offs, out):
 
     with (
         tc.tile_pool(name="held", bufs=1) as held,
-        tc.tile_pool(name="work", bufs=blocks * pieces) as work,
+        tc.tile_pool(name="work", bufs=blocks * pieces + LAST_PARTS) as work,
     ):
         zeros = held.tile([P, WARM_COLS], F32, name="zeros")
         nc.vector.memset(zeros[:], 0.0)
@@ -42,10 +43,15 @@ def tile_lookup_gate_silu_out_kernel(tc, tab, y, offs, out):
 
         for b in range(blocks):
             for k in range(pieces):
-                cols = slice(k * PIECE, (k + 1) * PIECE)
                 piece_offsets = offsets[:, k * piece_offset_cols : (k + 1) * piece_offset_cols]
                 gate = work.tile([P, PIECE], F32, name="gate")
                 nc.scalar.activation(gate[:], windows[b][:].indirect(piece_offsets), SILU)
-                x = work.tile([P, PIECE], F32, name="x")
-                nc.vector.tensor_tensor(x[:], gate[:], streams[b][:, cols], MULT)
-                nc.sync.dma_start(out[b * P : (b + 1) * P, cols], x[:])
+                is_last = b == blocks - 1 and k == pieces - 1
+                parts = LAST_PARTS if is_last else 1
+                width = PIECE // parts
+                for h in range(parts):
+                    part = slice(h * width, (h + 1) * width)
+                    cols = slice(k * PIECE + h * width, k * PIECE + (h + 1) * width)
+                    x = work.tile([P, width], F32, name="x", tag="x")
+                    nc.vector.tensor_tensor(x[:], gate[:, part], streams[b][:, cols], MULT)
+                    nc.sync.dma_start(out[b * P : (b + 1) * P, cols], x[:])

@@ -37,6 +37,7 @@ def tile_lookup_gate_silu_out_kernel(tc, tab, y, offs, out):
             window = held.tile([P, table_cols], F32, name=f"window{b}")
             nc.sync.dma_start(window[:], tab[b * P : (b + 1) * P, :])
             windows.append(window)
+        for b in range(blocks):
             stream = held.tile([P, n], F32, name=f"stream{b}")
             nc.sync.dma_start(stream[:], y[b * P : (b + 1) * P, :])
             streams.append(stream)

import concourse.mybir as mybir

F32 = mybir.dt.float32
U16 = mybir.dt.uint16
SILU = mybir.ActivationFunctionType.Silu
MULT = mybir.AluOpType.mult

P = 128
OFFSETS_PER_COL = 16
WARM_COLS = 8
LAST_PARTS = 2
PIECE = 512


def tile_lookup_gate_silu_out_kernel(tc, tab, y, offs, out):
    nc = tc.nc
    rows, table_cols = tab.shape
    n = y.shape[1]
    blocks = rows // P
    pieces = n // PIECE
    piece_offset_cols = PIECE // OFFSETS_PER_COL

    with (
        tc.tile_pool(name="held", bufs=1) as held,
        tc.tile_pool(name="work", bufs=blocks * pieces + LAST_PARTS) as work,
    ):
        zeros = held.tile([P, WARM_COLS], F32, name="zeros")
        nc.vector.memset(zeros[:], 0.0)
        warm = held.tile([P, WARM_COLS], F32, name="warm")
        nc.scalar.activation(warm[:], zeros[:], SILU)

        offsets = held.tile([P, n // OFFSETS_PER_COL], U16, name="offsets")
        nc.sync.dma_start(offsets[:], offs)
        windows = []
        streams = []
        for b in range(blocks):
            window = held.tile([P, table_cols], F32, name=f"window{b}")
            nc.sync.dma_start(window[:], tab[b * P : (b + 1) * P, :])
            windows.append(window)
        for b in range(blocks):
            stream = held.tile([P, n], F32, name=f"stream{b}")
            nc.sync.dma_start(stream[:], y[b * P : (b + 1) * P, :])
            streams.append(stream)

        for b in range(blocks):
            for k in range(pieces):
                piece_offsets = offsets[:, k * piece_offset_cols : (k + 1) * piece_offset_cols]
                gate = work.tile([P, PIECE], F32, name="gate")
                nc.scalar.activation(gate[:], windows[b][:].indirect(piece_offsets), SILU)
                is_last = b == blocks - 1 and k == pieces - 1
                parts = LAST_PARTS if is_last else 1
                width = PIECE // parts
                for h in range(parts):
                    part = slice(h * width, (h + 1) * width)
                    cols = slice(k * PIECE + h * width, k * PIECE + (h + 1) * width)
                    x = work.tile([P, width], F32, name="x", tag="x")
                    nc.vector.tensor_tensor(x[:], gate[:, part], streams[b][:, cols], MULT)
                    nc.sync.dma_start(out[b * P : (b + 1) * P, cols], x[:])
